import numpy as np
import ml_dtypes

BF16 = ml_dtypes.bfloat16


def bf(x):
    return np.asarray(x, np.float32).astype(BF16)


def f32(x):
    return np.asarray(x, np.float32)


def f64(x):
    return np.asarray(x).astype(np.float64)


def striped(idx):
    return np.tile(idx.reshape(-1, 16).T, (8, 1))


S, K, M, N, D = 1024, 512, 128, 128, 128


def setup_inputs():
    return {"table": bf(np.random.standard_normal((K, S))), "qw": bf(np.random.standard_normal((K, M)) / np.sqrt(K)), "kw": bf(np.random.standard_normal((K, M)) / np.sqrt(K)), "w": bf(np.random.standard_normal((K, D)) / np.sqrt(K)), "r": f32(0.5 * np.random.standard_normal((1, N))), "offs": striped(np.sort(np.random.permutation(S)[:N]))}


def reference(table, qw, kw, w, r, offs):
    idx = offs[:16].T.reshape(-1)
    x = f64(table)[:, idx]
    a = (f64(qw).T @ x).T @ (f64(kw).T @ x) / np.sqrt(M) + f64(r)
    a = np.exp(a - a.max(axis=1, keepdims=True))
    a = a / a.sum(axis=1, keepdims=True)
    return a @ (f64(w).T @ x).T

@@ -1,0 +1,91 @@
+import math
+
+import concourse.mybir as mybir
+from concourse.masks import make_identity
+
+P = 128
+BF16, F32, U16 = mybir.dt.bfloat16, mybir.dt.float32, mybir.dt.uint16
+FLOPS = 2 * 512 * 128 * 128 * 3 + 2 * 128 * 128 * 128 * 2
+
+
+def tile_rows_pruneattn_srt_kernel(tc, table, qw, kw, w, r, offs, out):
+    nc = tc.nc
+    K, S = table.shape
+    M = qw.shape[1]
+    N, D = out.shape
+    blocks = K // P
+
+    with (
+        tc.tile_pool(name="sbuf", bufs=1) as sbuf,
+        tc.psum_pool(name="psum", bufs=1) as psum,
+    ):
+        offsets = sbuf.tile([P, N // 16], U16)
+        nc.sync.dma_start(offsets[:], offs)
+
+        bias_row = sbuf.tile([1, N], F32)
+        nc.scalar.dma_start(bias_row[:], r)
+
+        weights = []
+        for name, source in (("qw", qw), ("kw", kw), ("w", w)):
+            tile = sbuf.tile([P, blocks, source.shape[1]], BF16, name=name)
+            nc.scalar.dma_start(tile[:], source.rearrange("(p b) m -> p b m", p=P))
+            weights.append(tile)
+
+        table_rows = table.rearrange("(p b) s -> p b s", p=P)
+        windows = []
+        for pair in range(blocks // 2):
+            tile = sbuf.tile([P, 2, S], BF16, name=f"table{pair}")
+            nc.sync.dma_start(tile[:], table_rows[:, 2 * pair : 2 * pair + 2, :])
+            windows += [tile[:, 0, :], tile[:, 1, :]]
+
+        identity = sbuf.tile([P, P], BF16)
+        make_identity(nc, identity[:])
+        ones_row = sbuf.tile([1, N], F32)
+        nc.vector.memset(ones_row[:], 1.0)
+
+        scores = psum.tile([N, N], F32)
+        nc.tensor.matmul(scores[:], ones_row[:], bias_row[:], start=True, stop=False)
+
+        q_sum = psum.tile([M, N], F32)
+        h_sum = psum.tile([M, N], F32)
+        v_sum = psum.tile([D, N], F32)
+        for pair in range(blocks // 2):
+            for total, weight in zip((q_sum, h_sum, v_sum), weights):
+                for b in (2 * pair, 2 * pair + 1):
+                    nc.tensor.matmul(
+                        total[:], weight[:, b, :], windows[b].indirect(offsets[:]),
+                        start=b == 0, stop=b == blocks - 1,
+                    )
+
+        q = sbuf.tile([M, N], BF16)
+        nc.vector.tensor_scalar(q[:], q_sum[:], 1.0 / math.sqrt(M), None, mybir.AluOpType.mult)
+        h = sbuf.tile([M, N], BF16)
+        nc.scalar.copy(h[:], h_sum[:])
+        nc.tensor.matmul(scores[:], q[:], h[:], start=False, stop=True)
+
+        v = sbuf.tile([D, N], BF16)
+        nc.scalar.copy(v[:], v_sum[:])
+        v_flipped = psum.tile([N, D], BF16)
+        nc.tensor.transpose(v_flipped[:], v[:], identity[:])
+
+        neg_max = sbuf.tile([N, 1], F32)
+        nc.vector.tensor_reduce(neg_max[:], scores[:], mybir.AxisListType.X, mybir.AluOpType.max, negate=True)
+        e = sbuf.tile([N, N], BF16)
+        e_sum = sbuf.tile([N, 1], F32)
+        nc.scalar.activation(e[:], scores[:], mybir.ActivationFunctionType.Exp, bias=neg_max[:], accum_out=e_sum[:])
+
+        v_rows = sbuf.tile([N, D], BF16)
+        nc.vector.tensor_copy(v_rows[:], v_flipped[:])
+
+        e_flipped = psum.tile([N, N], BF16)
+        nc.tensor.transpose(e_flipped[:], e[:], identity[:])
+        inv_sum = sbuf.tile([N, 1], F32)
+        nc.vector.reciprocal(inv_sum[:], e_sum[:])
+        e_keys = sbuf.tile([N, N], BF16)
+        nc.vector.tensor_copy(e_keys[:], e_flipped[:])
+
+        mixed = psum.tile([N, D], F32)
+        nc.tensor.matmul(mixed[:], e_keys[:], v_rows[:], start=True, stop=True)
+        result = sbuf.tile([N, D], F32)
+        nc.vector.tensor_scalar(result[:], mixed[:], inv_sum[:], None, mybir.AluOpType.mult)
+        nc.sync.dma_start(out, result[:])

@@ -19,9 +19,6 @@ def tile_rows_pruneattn_srt_kernel(tc, table, qw, kw, w, r, offs, out):
         tc.tile_pool(name="sbuf", bufs=1) as sbuf,
         tc.psum_pool(name="psum", bufs=1) as psum,
     ):
-        offsets = sbuf.tile([P, N // 16], U16)
-        nc.sync.dma_start(offsets[:], offs)
-
         bias_row = sbuf.tile([1, N], F32)
         nc.scalar.dma_start(bias_row[:], r)
 
@@ -32,11 +29,12 @@ def tile_rows_pruneattn_srt_kernel(tc, table, qw, kw, w, r, offs, out):
             weights.append(tile)
 
         table_rows = table.rearrange("(p b) s -> p b s", p=P)
-        windows = []
-        for pair in range(blocks // 2):
-            tile = sbuf.tile([P, 2, S], BF16, name=f"table{pair}")
-            nc.sync.dma_start(tile[:], table_rows[:, 2 * pair : 2 * pair + 2, :])
-            windows += [tile[:, 0, :], tile[:, 1, :]]
+        windows = [sbuf.tile([P, S], BF16, name=f"table{b}") for b in range(blocks)]
+        offsets = sbuf.tile([P, N // 16], U16)
+        nc.sync.dma_start(windows[0][:], table_rows[:, 0, :])
+        nc.sync.dma_start(offsets[:], offs)
+        for b in range(1, blocks):
+            nc.sync.dma_start(windows[b][:], table_rows[:, b, :])
 
         identity = sbuf.tile([P, P], BF16)
         make_identity(nc, identity[:])
@@ -49,18 +47,17 @@ def tile_rows_pruneattn_srt_kernel(tc, table, qw, kw, w, r, offs, out):
         q_sum = psum.tile([M, N], F32)
         h_sum = psum.tile([M, N], F32)
         v_sum = psum.tile([D, N], F32)
-        for pair in range(blocks // 2):
+        for b in range(blocks):
             for total, weight in zip((q_sum, h_sum, v_sum), weights):
-                for b in (2 * pair, 2 * pair + 1):
-                    nc.tensor.matmul(
-                        total[:], weight[:, b, :], windows[b].indirect(offsets[:]),
-                        start=b == 0, stop=b == blocks - 1,
-                    )
+                nc.tensor.matmul(
+                    total[:], weight[:, b, :], windows[b][:].indirect(offsets[:]),
+                    start=b == 0, stop=b == blocks - 1,
+                )
 
         q = sbuf.tile([M, N], BF16)
-        nc.vector.tensor_scalar(q[:], q_sum[:], 1.0 / math.sqrt(M), None, mybir.AluOpType.mult)
+        nc.scalar.activation(q[:], q_sum[:], mybir.ActivationFunctionType.Copy, scale=1.0 / math.sqrt(M))
         h = sbuf.tile([M, N], BF16)
-        nc.scalar.copy(h[:], h_sum[:])
+        nc.vector.tensor_copy(h[:], h_sum[:])
         nc.tensor.matmul(scores[:], q[:], h[:], start=False, stop=True)
 
         v = sbuf.tile([D, N], BF16)

import math

import concourse.mybir as mybir
from concourse.masks import make_identity

P = 128
BF16, F32, U16 = mybir.dt.bfloat16, mybir.dt.float32, mybir.dt.uint16
FLOPS = 2 * 512 * 128 * 128 * 3 + 2 * 128 * 128 * 128 * 2


def tile_rows_pruneattn_srt_kernel(tc, table, qw, kw, w, r, offs, out):
    nc = tc.nc
    K, S = table.shape
    M = qw.shape[1]
    N, D = out.shape
    blocks = K // P

    with (
        tc.tile_pool(name="sbuf", bufs=1) as sbuf,
        tc.psum_pool(name="psum", bufs=1) as psum,
    ):
        bias_row = sbuf.tile([1, N], F32)
        nc.scalar.dma_start(bias_row[:], r)

        weights = []
        for name, source in (("qw", qw), ("kw", kw), ("w", w)):
            tile = sbuf.tile([P, blocks, source.shape[1]], BF16, name=name)
            nc.scalar.dma_start(tile[:], source.rearrange("(p b) m -> p b m", p=P))
            weights.append(tile)

        table_rows = table.rearrange("(p b) s -> p b s", p=P)
        windows = [sbuf.tile([P, S], BF16, name=f"table{b}") for b in range(blocks)]
        offsets = sbuf.tile([P, N // 16], U16)
        nc.sync.dma_start(windows[0][:], table_rows[:, 0, :])
        nc.sync.dma_start(offsets[:], offs)
        for b in range(1, blocks):
            nc.sync.dma_start(windows[b][:], table_rows[:, b, :])

        identity = sbuf.tile([P, P], BF16)
        make_identity(nc, identity[:])
        ones_row = sbuf.tile([1, N], F32)
        nc.vector.memset(ones_row[:], 1.0)

        scores = psum.tile([N, N], F32)
        nc.tensor.matmul(scores[:], ones_row[:], bias_row[:], start=True, stop=False)

        q_sum = psum.tile([M, N], F32)
        h_sum = psum.tile([M, N], F32)
        v_sum = psum.tile([D, N], F32)
        for b in range(blocks):
            for total, weight in zip((q_sum, h_sum, v_sum), weights):
                nc.tensor.matmul(
                    total[:], weight[:, b, :], windows[b][:].indirect(offsets[:]),
                    start=b == 0, stop=b == blocks - 1,
                )

        q = sbuf.tile([M, N], BF16)
        nc.scalar.activation(q[:], q_sum[:], mybir.ActivationFunctionType.Copy, scale=1.0 / math.sqrt(M))
        h = sbuf.tile([M, N], BF16)
        nc.vector.tensor_copy(h[:], h_sum[:])
        nc.tensor.matmul(scores[:], q[:], h[:], start=False, stop=True)

        v = sbuf.tile([D, N], BF16)
        nc.scalar.copy(v[:], v_sum[:])
        v_flipped = psum.tile([N, D], BF16)
        nc.tensor.transpose(v_flipped[:], v[:], identity[:])

        neg_max = sbuf.tile([N, 1], F32)
        nc.vector.tensor_reduce(neg_max[:], scores[:], mybir.AxisListType.X, mybir.AluOpType.max, negate=True)
        e = sbuf.tile([N, N], BF16)
        e_sum = sbuf.tile([N, 1], F32)
        nc.scalar.activation(e[:], scores[:], mybir.ActivationFunctionType.Exp, bias=neg_max[:], accum_out=e_sum[:])

        v_rows = sbuf.tile([N, D], BF16)
        nc.vector.tensor_copy(v_rows[:], v_flipped[:])

        e_flipped = psum.tile([N, N], BF16)
        nc.tensor.transpose(e_flipped[:], e[:], identity[:])
        inv_sum = sbuf.tile([N, 1], F32)
        nc.vector.reciprocal(inv_sum[:], e_sum[:])
        e_keys = sbuf.tile([N, N], BF16)
        nc.vector.tensor_copy(e_keys[:], e_flipped[:])

        mixed = psum.tile([N, D], F32)
        nc.tensor.matmul(mixed[:], e_keys[:], v_rows[:], start=True, stop=True)
        result = sbuf.tile([N, D], F32)
        nc.vector.tensor_scalar(result[:], mixed[:], inv_sum[:], None, mybir.AluOpType.mult)
        nc.sync.dma_start(out, result[:])
